import numpy as np
import ml_dtypes


def mxq(x, axis, fmt="e4m3"):
    dtype, down = {"e4m3": (ml_dtypes.float8_e4m3fn, 7), "e5m2": (ml_dtypes.float8_e5m2, 14)}[fmt]
    v = np.moveaxis(np.asarray(x, np.float32).astype(ml_dtypes.bfloat16).astype(np.float64), axis, -1)
    blocks = v.reshape(v.shape[:-1] + (-1, 32))
    amax = np.abs(blocks).max(-1, keepdims=True)
    byte = np.maximum(np.where(amax > 0, np.frexp(amax)[1] - 1 + 127, 0) - down, 1)
    scale = np.exp2(byte - 127.0)
    codes = (blocks / scale).astype(np.float32).astype(dtype).astype(np.float64)
    return np.moveaxis((codes * scale).reshape(v.shape), -1, axis)


WIDE = False


def mx_kscale(k):
    if not WIDE:
        return np.ones(k)
    levels = np.array([10, -10, 5, -5, 0])
    if k % 512:
        return np.exp2(np.random.permutation(np.resize(levels, k // 32))).repeat(32)
    a = np.empty((k // 512, 16))
    for p in range(k // 512):
        a[p, :8] = np.random.permutation(np.resize(levels, 8))
        for g in range(8):
            far = levels[np.abs(levels - a[p, g]) >= 10]
            a[p, g + 8] = far[np.random.randint(len(far))]
    return np.exp2(a.ravel()).repeat(32)


def f64(x):
    return np.asarray(x).astype(np.float64)


def striped(idx):
    return np.tile(idx.reshape(-1, 16).T, (8, 1)).astype(np.uint16)


def unstriped(offs):
    return offs[:16].T.reshape(-1).astype(np.int64)


def pack_weight(w):
    k, n = w.shape
    w = f64(np.asarray(w, np.float32).astype(ml_dtypes.bfloat16)).reshape(k // 32, 32, n)
    amax = np.abs(w).max(1)
    byte = np.clip(np.where(amax > 0, np.frexp(amax)[1] - 1 + 127 - 7, 1), 1, 254)
    scaled = (w * np.exp2(127.0 - byte)[:, None, :]).reshape(k, n).astype(np.float32)
    words = np.ascontiguousarray(scaled.reshape(k // 512, 128, 4, n).transpose(0, 1, 3, 2)).astype(ml_dtypes.float8_e4m3fn).view(np.uint8)
    return words, np.ascontiguousarray(byte.astype(np.uint8).reshape(k // 512, 16, n))


def unpack_weight(words, scales):
    g, p, n, _ = words.shape
    vals = np.ascontiguousarray(words).view(ml_dtypes.float8_e4m3fn).astype(np.float64) * np.repeat(np.exp2(scales.astype(np.float64) - 127.0), 8, axis=1)[..., None]
    return vals.transpose(0, 1, 3, 2).reshape(g * 512, n)


K, T, S, D, H, N = 512, 2048, 512, 4, 512, 256


def setup_inputs():
    n = np.random.standard_normal
    s = mx_kscale(K)[:, None]
    u = mx_kscale(H)
    packed_xT = pack_weight(n((K, T)) * s)
    return {
        "x_words": packed_xT[0],
        "x_scales": packed_xT[1],
        "w1": (n((K, H)) / np.sqrt(K) / s).astype(np.float32),
        "w2": (n((K, H)) / np.sqrt(K) / s).astype(np.float32),
        "unit": (np.random.uniform(0.5, 1.5, (H, 1)) * u[:, None]).astype(np.float32),
        "wn": (np.random.uniform(0.0, 2.0, (H, N)) / H / u[:, None]).astype(np.float32),
        "wd": (np.random.uniform(0.0, 2.0, (H, N)) / H / u[:, None]).astype(np.float32),
        "rmax": (np.random.uniform(0.5, 3.0, (N, 1))).astype(np.float32),
        "half": (np.random.uniform(0.3, 1.5, (N, 1))).astype(np.float32),
        "offs": striped(np.random.permutation(T)[:S]),
    }


def reference(x_words, x_scales, w1, w2, unit, wn, wd, rmax, half, offs):
    xq = unpack_weight(x_words, x_scales)[:, unstriped(offs)]
    e1 = f64(unit) * (((mxq(f64(w1), 0, "e4m3").T @ xq)) ** 2 + ((mxq(f64(w2), 0, "e4m3").T @ xq)) ** 2)
    e1q = mxq(e1, 0, "e4m3")
    drive = mxq(f64(wd), 0, "e4m3").T @ e1q
    norm1 = mxq(f64(wn), 0, "e4m3").T @ e1q
    rr = np.sqrt((f64(rmax) * drive) / (norm1 + f64(half)))
    mr = rr.reshape(len(rr), -1, D).mean(axis=2)
    return rr - np.repeat(mr, D, axis=1)

@@ -1,0 +1,206 @@
+from contextlib import ExitStack
+
+import concourse.mybir as mybir
+from concourse.masks import make_identity
+
+K, T, S, D, H, N = 512, 2048, 512, 4, 512, 256
+FLOPS = 2 * K * H * S * 2 + 2 * H * N * S * 2
+
+F32 = mybir.dt.float32
+BF16 = mybir.dt.bfloat16
+I32 = mybir.dt.int32
+U32 = mybir.dt.uint32
+U16 = mybir.dt.uint16
+U8 = mybir.dt.uint8
+FP8X4 = mybir.dt.float8_e4m3fn_x4
+ACT = mybir.ActivationFunctionType
+ALU = mybir.AluOpType
+AX = mybir.AxisListType
+
+P = 128
+PACK = 4
+HALF = 256
+TINY = 2.0 ** -84
+C2 = 2.0 ** (-2.0 / 3.0)
+CHUNKS = ((0,2),(2,2))
+
+
+def tile_picked_yenergy_dev_p_kernel(tc, x_words, x_scales, w1, w2, unit, wn, wd, rmax, half, offs, out):
+    nc = tc.nc
+    with ExitStack() as ctx:
+        keep = ctx.enter_context(tc.tile_pool(name="keep", bufs=1))
+        psum = ctx.enter_context(tc.psum_pool(name="psum", bufs=1))
+
+        offsets = keep.tile([P, S // 16], U16, name="offsets")
+        table_words = keep.tile([P, T], I32, name="table_words", align_bytes=64)
+        table_scales = keep.tile([P, T], U8, name="table_scales", align_bytes=64)
+        ident = keep.tile([P, P], F32, name="ident")
+        tiny = keep.tile([P, 1], F32, name="tiny")
+        warm = keep.tile([P, 1], F32, name="warm")
+        unit_sb = keep.tile([P, PACK], F32, name="unit_sb")
+        rmax_sb = keep.tile([P, 2], F32, name="rmax_sb")
+        half_sb = keep.tile([P, 2], F32, name="half_sb")
+
+        nc.gpsimd.memset(table_scales[:].bitcast(I32), 0)
+        nc.vector.memset(tiny[:], TINY)
+        nc.scalar.activation(warm[:], tiny[:], ACT.Abs_reciprocal_sqrt)
+        make_identity(nc, ident[:])
+
+        def load_rows(name, w, c0, width):
+            raw = keep.tile([P, PACK, width], F32, name=name)
+            nc.sync.dma_start(out=raw[:], in_=w.rearrange("(p j) c -> p j c", j=PACK)[:, :, c0 : c0 + width])
+            return raw
+
+        nc.sync.dma_start(offsets[:], offs)
+        raw1 = load_rows("raw1", w1, 0, H)
+        for q in range(4):
+            nc.sync.dma_start(
+                out=table_scales[32 * q : 32 * q + 4, :].bitcast(I32),
+                in_=x_scales[0][4 * q : 4 * q + 4, :].bitcast(I32),
+            )
+        nc.sync.dma_start(out=table_words[:], in_=x_words[0].rearrange("p n t -> p (n t)").bitcast(I32))
+        raw2 = [load_rows("raw2_%d" % h, w2, h * HALF, HALF) for h in range(2)]
+        nc.sync.dma_start(out=unit_sb[:], in_=unit.rearrange("(p t) o -> p (t o)", t=PACK))
+        rawd = load_rows("rawd", wd, 0, N)
+        rawn = load_rows("rawn", wn, 0, N)
+        with nc.allow_non_contiguous_dma(reason="one value a partition"):
+            nc.sync.dma_start(out=rmax_sb[:], in_=rmax.rearrange("(m p) o -> p (m o)", p=P))
+            nc.sync.dma_start(out=half_sb[:], in_=half.rearrange("(m p) o -> p (m o)", p=P))
+
+        def weave(copy, name, raw, c0, width):
+            woven = keep.tile([P, width * PACK], BF16, name=name, align_bytes=64)
+            copy(
+                woven[:].rearrange("p (c i j) -> p c j i", i=4, j=PACK),
+                raw[:, :, c0 : c0 + width].rearrange("p j (c i) -> p c j i", i=4),
+            )
+            return woven
+
+        def planes(name, width):
+            codes = keep.tile([P, width], U32, name=name + "_codes", align_bytes=64)
+            scales = keep.tile([P, width], U8, name=name + "_scales", align_bytes=64)
+            return codes, scales
+
+        def quantize(dst, c0, width, woven):
+            nc.vector.quantize_mx(
+                out=dst[0][:, c0 : c0 + width].bitcast(FP8X4), scales=dst[1][:, c0 : c0 + width], in_=woven
+            )
+
+        def mx(acc, lhs, l0, rhs, r0, width):
+            nc.tensor.matmul_mx(
+                out=acc,
+                lhsT=lhs[0][:, l0 : l0 + P].bitcast(FP8X4),
+                lhsT_scale=lhs[1][:, l0 : l0 + P],
+                rhs=rhs[0][:, r0 : r0 + width].bitcast(FP8X4),
+                rhs_scale=rhs[1][:, r0 : r0 + width],
+                start=True,
+                stop=True,
+            )
+
+        picked_words = keep.tile([P, S], U32, name="picked_words", align_bytes=64)
+        picked_scales = keep.tile([P, S], U8, name="picked_scales", align_bytes=64)
+        picked = (picked_words, picked_scales)
+        nc.vector.tensor_copy(picked_scales[:], table_scales[:].indirect(offsets[:]))
+
+        q1 = planes("q1", H)
+        woven1 = [
+            weave(nc.vector.tensor_copy, "woven1_0", raw1, 0, HALF),
+            weave(nc.scalar.copy, "woven1_1", raw1, HALF, HALF),
+        ]
+        for h in range(2):
+            quantize(q1, h * HALF, HALF, woven1[h][:])
+        for h in range(2):
+            nc.vector.tensor_copy(
+                picked_words[:, h * HALF : (h + 1) * HALF],
+                table_words[:].bitcast(U32).indirect(offsets[:, h * 16 : (h + 1) * 16]),
+            )
+
+        def squared(name, i, q):
+            acc = psum.tile([P, H], F32, name="filters", bufs=2)
+            mx(acc[:], picked, i * P, q, 0, H)
+            sq = keep.tile([P, PACK, P], F32, name=name)
+            nc.scalar.activation(sq[:], acc[:].rearrange("p (m t) -> p t m", t=PACK), ACT.Square)
+            return sq
+
+        totals = []
+        for i in range(4):
+            sq1 = squared("sq1_%d" % i, i, q1)
+            total = psum.tile([P, PACK, P], F32, name="total", bufs=4)
+            for t in range(PACK):
+                nc.tensor.matmul(total[:, t, :], sq1[:, t, :], ident[:], start=(t == 0), stop=False, is_transpose=True)
+            totals.append(total)
+
+        q2 = planes("q2", H)
+        for h in range(2):
+            woven2 = weave(nc.vector.tensor_copy, "woven2_%d" % h, raw2[h], 0, HALF)
+            quantize(q2, h * HALF, HALF, woven2[:])
+        qd = planes("qd", N)
+        qn = planes("qn", N)
+        wovend = weave(nc.vector.tensor_copy, "wovend", rawd, 0, N)
+        wovenn = weave(nc.vector.tensor_copy, "wovenn", rawn, 0, N)
+        quantize(qd, 0, N, wovend[:])
+        quantize(qn, 0, N, wovenn[:])
+
+        def energy(i, qe, c0):
+            sq2 = squared("sq2_%d" % i, i, q2)
+            total = totals[i]
+            for t in range(PACK):
+                nc.tensor.matmul(
+                    total[:, t, :], sq2[:, t, :], ident[:], start=False, stop=(t == PACK - 1), is_transpose=True
+                )
+            e1 = keep.tile([P, P, PACK], BF16, name="e1_%d" % i, align_bytes=64)
+            nc.vector.tensor_tensor(
+                e1[:],
+                total[:].rearrange("p t n -> p n t"),
+                unit_sb[:].unsqueeze(1).to_broadcast([P, P, PACK]),
+                ALU.mult,
+            )
+            quantize(qe, c0, P, e1[:].rearrange("p n t -> p (n t)"))
+
+        def rates(c, qe, c0, width):
+            drive = psum.tile([P, 2, width], F32, name="cells", bufs=2)
+            norm = psum.tile([P, 2, width], F32, name="cells", bufs=2)
+            for m in range(2):
+                mx(drive[:, m, :], qd, m * P, qe, 0, width)
+            for m in range(2):
+                mx(norm[:, m, :], qn, m * P, qe, 0, width)
+
+            def work(name):
+                return keep.tile([P, 2 * width], F32, name="%s_%d" % (name, c))
+
+            num, prod, inv, inv2, first, check, rate, res = [
+                work(name) for name in ("num", "prod", "inv", "inv2", "first", "check", "rate", "res")
+            ]
+            for m in range(2):
+                cols = slice(m * width, (m + 1) * width)
+                nc.scalar.activation(num[:, cols], drive[:, m, :], ACT.Abs, scale=rmax_sb[:, m : m + 1])
+                nc.vector.scalar_tensor_tensor(
+                    prod[:, cols], norm[:, m, :], half_sb[:, m : m + 1], num[:, cols], ALU.add, ALU.mult
+                )
+            nc.scalar.activation(inv[:], prod[:], ACT.Abs_reciprocal_sqrt, bias=tiny[:], scale=1.0 / C2)
+            nc.scalar.activation(inv2[:], inv[:], ACT.Square)
+            nc.vector.tensor_tensor(first[:], num[:], inv[:], ALU.mult)
+            nc.vector.tensor_tensor(check[:], prod[:], inv2[:], ALU.mult)
+            nc.vector.scalar_tensor_tensor(rate[:], check[:], 3.0 * C2, first[:], ALU.subtract, ALU.mult)
+            groups = 2 * width // D
+            sums = keep.tile([P, groups], F32, name="sums_%d" % c)
+            by_group = "p (v d) -> p v d"
+            nc.vector.tensor_reduce(sums[:], rate[:].rearrange(by_group, d=D), AX.X, ALU.add)
+            nc.vector.scalar_tensor_tensor(
+                res[:].rearrange(by_group, d=D),
+                sums[:].unsqueeze(2).to_broadcast([P, groups, D]),
+                1.0 / D,
+                rate[:].rearrange(by_group, d=D),
+                ALU.mult,
+                ALU.subtract,
+            )
+            nc.sync.dma_start(
+                out=out.rearrange("(m p) n -> p m n", p=P)[:, :, c0 : c0 + width],
+                in_=res[:].rearrange("p (m n) -> p m n", m=2),
+            )
+
+        qes = [planes("qe_%d" % c, n * P) for c, (i0, n) in enumerate(CHUNKS)]
+        for c, (i0, n) in enumerate(CHUNKS):
+            for i in range(n):
+                energy(i0 + i, qes[c], i * P)
+        for c, (i0, n) in enumerate(CHUNKS):
+            rates(c, qes[c], i0 * P, n * P)

@@ -1,7 +1,6 @@
 from contextlib import ExitStack
 
 import concourse.mybir as mybir
-from concourse.masks import make_identity
 
 K, T, S, D, H, N = 512, 2048, 512, 4, 512, 256
 FLOPS = 2 * K * H * S * 2 + 2 * H * N * S * 2
@@ -22,29 +21,25 @@ PACK = 4
 HALF = 256
 TINY = 2.0 ** -84
 C2 = 2.0 ** (-2.0 / 3.0)
-CHUNKS = ((0,2),(2,2))
+CHUNKS = ((0,128),(128,128),(256,256))
 
 
 def tile_picked_yenergy_dev_p_kernel(tc, x_words, x_scales, w1, w2, unit, wn, wd, rmax, half, offs, out):
     nc = tc.nc
     with ExitStack() as ctx:
         keep = ctx.enter_context(tc.tile_pool(name="keep", bufs=1))
-        psum = ctx.enter_context(tc.psum_pool(name="psum", bufs=1))
+        psum = ctx.enter_context(tc.psum_pool(name="psum", bufs=4))
 
         offsets = keep.tile([P, S // 16], U16, name="offsets")
         table_words = keep.tile([P, T], I32, name="table_words", align_bytes=64)
-        table_scales = keep.tile([P, T], U8, name="table_scales", align_bytes=64)
-        ident = keep.tile([P, P], F32, name="ident")
+        table_scales = keep.tile([P, T], U8, name="table_scales", tag="early", align_bytes=64)
         tiny = keep.tile([P, 1], F32, name="tiny")
-        warm = keep.tile([P, 1], F32, name="warm")
         unit_sb = keep.tile([P, PACK], F32, name="unit_sb")
         rmax_sb = keep.tile([P, 2], F32, name="rmax_sb")
         half_sb = keep.tile([P, 2], F32, name="half_sb")
 
-        nc.gpsimd.memset(table_scales[:].bitcast(I32), 0)
-        nc.vector.memset(tiny[:], TINY)
-        nc.scalar.activation(warm[:], tiny[:], ACT.Abs_reciprocal_sqrt)
-        make_identity(nc, ident[:])
+        nc.vector.memset(table_scales[:].bitcast(I32), 0)
+        nc.gpsimd.memset(tiny[:], TINY)
 
         def load_rows(name, w, c0, width):
             raw = keep.tile([P, PACK, width], F32, name=name)
@@ -52,6 +47,7 @@ def tile_picked_yenergy_dev_p_kernel(tc, x_words, x_scales, w1, w2, unit, wn, wd
             return raw
 
         nc.sync.dma_start(offsets[:], offs)
+        nc.sync.dma_start(out=unit_sb[:], in_=unit.rearrange("(p t) o -> p (t o)", t=PACK))
         raw1 = load_rows("raw1", w1, 0, H)
         for q in range(4):
             nc.sync.dma_start(
@@ -60,23 +56,31 @@ def tile_picked_yenergy_dev_p_kernel(tc, x_words, x_scales, w1, w2, unit, wn, wd
             )
         nc.sync.dma_start(out=table_words[:], in_=x_words[0].rearrange("p n t -> p (n t)").bitcast(I32))
         raw2 = [load_rows("raw2_%d" % h, w2, h * HALF, HALF) for h in range(2)]
-        nc.sync.dma_start(out=unit_sb[:], in_=unit.rearrange("(p t) o -> p (t o)", t=PACK))
         rawd = load_rows("rawd", wd, 0, N)
         rawn = load_rows("rawn", wn, 0, N)
         with nc.allow_non_contiguous_dma(reason="one value a partition"):
             nc.sync.dma_start(out=rmax_sb[:], in_=rmax.rearrange("(m p) o -> p (m o)", p=P))
             nc.sync.dma_start(out=half_sb[:], in_=half.rearrange("(m p) o -> p (m o)", p=P))
 
-        def weave(copy, name, raw, c0, width):
-            woven = keep.tile([P, width * PACK], BF16, name=name, align_bytes=64)
-            copy(
-                woven[:].rearrange("p (c i j) -> p c j i", i=4, j=PACK),
-                raw[:, :, c0 : c0 + width].rearrange("p j (c i) -> p c j i", i=4),
-            )
-            return woven
+        def minus_root_of_ratio(name, width, num, prod):
+            inv, inv2, first, check, root = [
+                keep.tile([P, width], F32, name=name + part) for part in ("_inv", "_inv2", "_first", "_check", "_root")
+            ]
+            nc.scalar.activation(inv[:], prod, ACT.Abs_reciprocal_sqrt, bias=tiny[:], scale=1.0 / C2)
+            nc.scalar.activation(inv2[:], inv[:], ACT.Square)
+            nc.vector.tensor_tensor(first[:], num, inv[:], ALU.mult)
+            nc.vector.tensor_tensor(check[:], prod, inv2[:], ALU.mult)
+            nc.vector.scalar_tensor_tensor(root[:], check[:], 3.0 * C2, first[:], ALU.subtract, ALU.mult)
+            return root
 
-        def planes(name, width):
-            codes = keep.tile([P, width], U32, name=name + "_codes", align_bytes=64)
+        unit_abs = keep.tile([P, PACK], F32, name="unit_abs")
+        unit_sign = keep.tile([P, PACK], F32, name="unit_sign")
+        nc.vector.scalar_tensor_tensor(unit_abs[:], unit_sb[:], -1.0, unit_sb[:], ALU.mult, ALU.max)
+        unit_root = minus_root_of_ratio("unit", PACK, unit_abs[:], unit_abs[:])
+        nc.scalar.activation(unit_sign[:], unit_sb[:], ACT.Sign)
+
+        def planes(name, width, tag=None):
+            codes = keep.tile([P, width], U32, name=name + "_codes", tag=tag or name, align_bytes=64)
             scales = keep.tile([P, width], U8, name=name + "_scales", align_bytes=64)
             return codes, scales
 
@@ -96,93 +100,84 @@ def tile_picked_yenergy_dev_p_kernel(tc, x_words, x_scales, w1, w2, unit, wn, wd
                 stop=True,
             )
 
+        def deal(copy, woven, m0, count, raw, c0):
+            copy(
+                woven[:, :, m0 : m0 + count, :].rearrange("p t m j -> p m t j"),
+                raw[:, :, c0 : c0 + PACK * count].rearrange("p j (m t) -> p m t j", t=PACK),
+            )
+
+        def quantize_dealt(name, woven, tag):
+            q = planes(name, H, tag)
+            quantize(q, 0, H, woven[:].rearrange("p t m j -> p (t m j)"))
+            return q
+
         picked_words = keep.tile([P, S], U32, name="picked_words", align_bytes=64)
         picked_scales = keep.tile([P, S], U8, name="picked_scales", align_bytes=64)
         picked = (picked_words, picked_scales)
         nc.vector.tensor_copy(picked_scales[:], table_scales[:].indirect(offsets[:]))
 
-        q1 = planes("q1", H)
-        woven1 = [
-            weave(nc.vector.tensor_copy, "woven1_0", raw1, 0, HALF),
-            weave(nc.scalar.copy, "woven1_1", raw1, HALF, HALF),
-        ]
-        for h in range(2):
-            quantize(q1, h * HALF, HALF, woven1[h][:])
-        for h in range(2):
-            nc.vector.tensor_copy(
-                picked_words[:, h * HALF : (h + 1) * HALF],
-                table_words[:].bitcast(U32).indirect(offsets[:, h * 16 : (h + 1) * 16]),
-            )
+        woven1 = keep.tile([P, PACK, P, PACK], BF16, name="woven1", align_bytes=64)
+        deal(nc.vector.tensor_copy, woven1, 0, 64, raw1, 0)
+        deal(nc.scalar.copy, woven1, 64, P - 64, raw1, PACK * 64)
+        q1 = quantize_dealt("q1", woven1, "early")
+        nc.vector.tensor_copy(picked_words[:], table_words[:].bitcast(U32).indirect(offsets[:]))
 
-        def squared(name, i, q):
-            acc = psum.tile([P, H], F32, name="filters", bufs=2)
-            mx(acc[:], picked, i * P, q, 0, H)
-            sq = keep.tile([P, PACK, P], F32, name=name)
-            nc.scalar.activation(sq[:], acc[:].rearrange("p (m t) -> p t m", t=PACK), ACT.Square)
-            return sq
+        woven2 = keep.tile([P, PACK, P, PACK], BF16, name="woven2", align_bytes=64)
+        deal(nc.scalar.copy, woven2, 0, 64, raw2[0], 0)
+        deal(nc.vector.tensor_copy, woven2, 64, 40, raw2[1], 0)
+        deal(nc.scalar.copy, woven2, 64 + 40, 64 - 40, raw2[1], PACK * 40)
+        q2 = quantize_dealt("q2", woven2, "q2")
 
-        totals = []
-        for i in range(4):
-            sq1 = squared("sq1_%d" % i, i, q1)
-            total = psum.tile([P, PACK, P], F32, name="total", bufs=4)
-            for t in range(PACK):
-                nc.tensor.matmul(total[:, t, :], sq1[:, t, :], ident[:], start=(t == 0), stop=False, is_transpose=True)
-            totals.append(total)
+        sq1 = keep.tile([P, PACK, S], F32, name="sq1")
+        for t in range(PACK):
+            acc = psum.tile([P, S], F32, name="filters")
+            mx(acc[:], q1, t * P, picked, 0, S)
+            nc.scalar.activation(sq1[:, t, :], acc[:], ACT.Square, scale=unit_root[:, t : t + 1])
 
-        q2 = planes("q2", H)
-        for h in range(2):
-            woven2 = weave(nc.vector.tensor_copy, "woven2_%d" % h, raw2[h], 0, HALF)
-            quantize(q2, h * HALF, HALF, woven2[:])
-        qd = planes("qd", N)
-        qn = planes("qn", N)
-        wovend = weave(nc.vector.tensor_copy, "wovend", rawd, 0, N)
-        wovenn = weave(nc.vector.tensor_copy, "wovenn", rawn, 0, N)
-        quantize(qd, 0, N, wovend[:])
-        quantize(qn, 0, N, wovenn[:])
 
-        def energy(i, qe, c0):
-            sq2 = squared("sq2_%d" % i, i, q2)
-            total = totals[i]
-            for t in range(PACK):
-                nc.tensor.matmul(
-                    total[:, t, :], sq2[:, t, :], ident[:], start=False, stop=(t == PACK - 1), is_transpose=True
-                )
-            e1 = keep.tile([P, P, PACK], BF16, name="e1_%d" % i, align_bytes=64)
+        def signed(name, raw):
+            woven = keep.tile([P, N * PACK], BF16, name=name + "_woven", align_bytes=64)
             nc.vector.tensor_tensor(
-                e1[:],
-                total[:].rearrange("p t n -> p n t"),
-                unit_sb[:].unsqueeze(1).to_broadcast([P, P, PACK]),
+                woven[:].rearrange("p (c i j) -> p c j i", i=4, j=PACK),
+                raw[:].rearrange("p j (c i) -> p c j i", i=4),
+                unit_sign[:].unsqueeze(1).unsqueeze(3).to_broadcast([P, N // 4, PACK, 4]),
                 ALU.mult,
             )
-            quantize(qe, c0, P, e1[:].rearrange("p n t -> p (n t)"))
+            q = planes(name, N)
+            quantize(q, 0, N, woven[:])
+            return q
 
-        def rates(c, qe, c0, width):
-            drive = psum.tile([P, 2, width], F32, name="cells", bufs=2)
-            norm = psum.tile([P, 2, width], F32, name="cells", bufs=2)
-            for m in range(2):
-                mx(drive[:, m, :], qd, m * P, qe, 0, width)
-            for m in range(2):
-                mx(norm[:, m, :], qn, m * P, qe, 0, width)
+        qd = signed("qd", rawd)
 
-            def work(name):
-                return keep.tile([P, 2 * width], F32, name="%s_%d" % (name, c))
+        def energy(c, c0, width):
+            sq2 = keep.tile([P, PACK, width], F32, name="sq2_%d" % c)
+            per_bank = S // width
+            for t0 in range(0, PACK, per_bank):
+                acc = psum.tile([P, per_bank, width], F32, name="filters")
+                for t in range(per_bank):
+                    mx(acc[:, t, :], q2, (t0 + t) * P, picked, c0, width)
+                for t in range(per_bank):
+                    nc.scalar.activation(
+                        sq2[:, t0 + t, :], acc[:, t, :], ACT.Square, scale=unit_root[:, t0 + t : t0 + t + 1]
+                    )
+            e1 = keep.tile([P, width * PACK], BF16, name="e1_%d" % c, align_bytes=64)
+            by_four = "p t (c i) -> p c t i"
+            nc.vector.tensor_tensor(
+                e1[:].rearrange("p (c i t) -> p c t i", i=4, t=PACK),
+                sq1[:, :, c0 : c0 + width].rearrange(by_four, i=4),
+                sq2[:].rearrange(by_four, i=4),
+                ALU.add,
+            )
+            qe = planes("qe_%d" % c, width)
+            quantize(qe, 0, width, e1[:])
+            return qe
 
-            num, prod, inv, inv2, first, check, rate, res = [
-                work(name) for name in ("num", "prod", "inv", "inv2", "first", "check", "rate", "res")
-            ]
-            for m in range(2):
-                cols = slice(m * width, (m + 1) * width)
-                nc.scalar.activation(num[:, cols], drive[:, m, :], ACT.Abs, scale=rmax_sb[:, m : m + 1])
-                nc.vector.scalar_tensor_tensor(
-                    prod[:, cols], norm[:, m, :], half_sb[:, m : m + 1], num[:, cols], ALU.add, ALU.mult
-                )
-            nc.scalar.activation(inv[:], prod[:], ACT.Abs_reciprocal_sqrt, bias=tiny[:], scale=1.0 / C2)
-            nc.scalar.activation(inv2[:], inv[:], ACT.Square)
-            nc.vector.tensor_tensor(first[:], num[:], inv[:], ALU.mult)
-            nc.vector.tensor_tensor(check[:], prod[:], inv2[:], ALU.mult)
-            nc.vector.scalar_tensor_tensor(rate[:], check[:], 3.0 * C2, first[:], ALU.subtract, ALU.mult)
-            groups = 2 * width // D
-            sums = keep.tile([P, groups], F32, name="sums_%d" % c)
+        def finish(name, num, prod, ms, c0, width):
+            total = len(ms) * width
+            rate = minus_root_of_ratio(name, total, num, prod)
+            groups = total // D
+            sums = keep.tile([P, groups], F32, name=name + "_sums")
+            res = keep.tile([P, total], F32, name=name + "_res")
             by_group = "p (v d) -> p v d"
             nc.vector.tensor_reduce(sums[:], rate[:].rearrange(by_group, d=D), AX.X, ALU.add)
             nc.vector.scalar_tensor_tensor(
@@ -194,13 +189,30 @@ def tile_picked_yenergy_dev_p_kernel(tc, x_words, x_scales, w1, w2, unit, wn, wd
                 ALU.subtract,
             )
             nc.sync.dma_start(
-                out=out.rearrange("(m p) n -> p m n", p=P)[:, :, c0 : c0 + width],
-                in_=res[:].rearrange("p (m n) -> p m n", m=2),
+                out=out.rearrange("(m p) n -> p m n", p=P)[:, ms[0] : ms[-1] + 1, c0 : c0 + width],
+                in_=res[:].rearrange("p (m n) -> p m n", m=len(ms)),
             )
 
-        qes = [planes("qe_%d" % c, n * P) for c, (i0, n) in enumerate(CHUNKS)]
-        for c, (i0, n) in enumerate(CHUNKS):
-            for i in range(n):
-                energy(i0 + i, qes[c], i * P)
-        for c, (i0, n) in enumerate(CHUNKS):
-            rates(c, qes[c], i0 * P, n * P)
+        def rates(c, qe, c0, width, parts):
+            num = keep.tile([P, 2 * width], F32, name="num_%d" % c)
+            prod = keep.tile([P, 2 * width], F32, name="prod_%d" % c)
+            drive = [psum.tile([P, width], F32, name="filters") for m in range(2)]
+            norm = [psum.tile([P, width], F32, name="cells") for m in range(2)]
+            for m in range(2):
+                mx(drive[m][:], qd, m * P, qe, 0, width)
+                mx(norm[m][:], qn, m * P, qe, 0, width)
+            for ms in parts:
+                for m in ms:
+                    cols = slice(m * width, (m + 1) * width)
+                    nc.scalar.activation(num[:, cols], drive[m][:], ACT.Abs, scale=rmax_sb[:, m : m + 1])
+                    nc.vector.scalar_tensor_tensor(
+                        prod[:, cols], norm[m][:], half_sb[:, m : m + 1], num[:, cols], ALU.add, ALU.mult
+                    )
+            for ms in parts:
+                cols = slice(ms[0] * width, (ms[-1] + 1) * width)
+                finish("rate_%d_%d" % (c, ms[0]), num[:, cols], prod[:, cols], ms, c0, width)
+
+        qn = signed("qn", rawn)
+        qes = [energy(c, c0, width) for c, (c0, width) in enumerate(CHUNKS)]
+        for c, (c0, width) in enumerate(CHUNKS):
+            rates(c, qes[c], c0, width, [(0, 1)] if width == P else [(0,), (1,)])

@@ -106,8 +106,8 @@ def tile_picked_yenergy_dev_p_kernel(tc, x_words, x_scales, w1, w2, unit, wn, wd
                 raw[:, :, c0 : c0 + PACK * count].rearrange("p j (m t) -> p m t j", t=PACK),
             )
 
-        def quantize_dealt(name, woven, tag):
-            q = planes(name, H, tag)
+        def quantize_dealt(name, woven):
+            q = planes(name, H, "early")
             quantize(q, 0, H, woven[:].rearrange("p t m j -> p (t m j)"))
             return q
 
@@ -117,16 +117,10 @@ def tile_picked_yenergy_dev_p_kernel(tc, x_words, x_scales, w1, w2, unit, wn, wd
         nc.vector.tensor_copy(picked_scales[:], table_scales[:].indirect(offsets[:]))
 
         woven1 = keep.tile([P, PACK, P, PACK], BF16, name="woven1", align_bytes=64)
-        deal(nc.vector.tensor_copy, woven1, 0, 64, raw1, 0)
-        deal(nc.scalar.copy, woven1, 64, P - 64, raw1, PACK * 64)
-        q1 = quantize_dealt("q1", woven1, "early")
+        deal(nc.vector.tensor_copy, woven1, 0, 16, raw1, 0)
+        deal(nc.scalar.copy, woven1, 16, P - 16, raw1, PACK * 16)
+        q1 = quantize_dealt("q1", woven1)
         nc.vector.tensor_copy(picked_words[:], table_words[:].bitcast(U32).indirect(offsets[:]))
-
-        woven2 = keep.tile([P, PACK, P, PACK], BF16, name="woven2", align_bytes=64)
-        deal(nc.scalar.copy, woven2, 0, 64, raw2[0], 0)
-        deal(nc.vector.tensor_copy, woven2, 64, 40, raw2[1], 0)
-        deal(nc.scalar.copy, woven2, 64 + 40, 64 - 40, raw2[1], PACK * 40)
-        q2 = quantize_dealt("q2", woven2, "q2")
 
         sq1 = keep.tile([P, PACK, S], F32, name="sq1")
         for t in range(PACK):
@@ -134,6 +128,12 @@ def tile_picked_yenergy_dev_p_kernel(tc, x_words, x_scales, w1, w2, unit, wn, wd
             mx(acc[:], q1, t * P, picked, 0, S)
             nc.scalar.activation(sq1[:, t, :], acc[:], ACT.Square, scale=unit_root[:, t : t + 1])
 
+        woven2 = keep.tile([P, PACK, P, PACK], BF16, name="woven2", align_bytes=64)
+        q2 = planes("q2", H)
+        for h in range(2):
+            deal(nc.vector.tensor_copy, woven2, h * 64, 64, raw2[h], 0)
+            for t in range(PACK):
+                quantize(q2, t * P + h * 64, 64, woven2[:, t, h * 64 : (h + 1) * 64, :].rearrange("p m j -> p (m j)"))
 
         def signed(name, raw):
             woven = keep.tile([P, N * PACK], BF16, name=name + "_woven", align_bytes=64)

@@ -46,9 +46,9 @@ def tile_picked_yenergy_dev_p_kernel(tc, x_words, x_scales, w1, w2, unit, wn, wd
             nc.sync.dma_start(out=raw[:], in_=w.rearrange("(p j) c -> p j c", j=PACK)[:, :, c0 : c0 + width])
             return raw
 
-        nc.sync.dma_start(offsets[:], offs)
         nc.sync.dma_start(out=unit_sb[:], in_=unit.rearrange("(p t) o -> p (t o)", t=PACK))
         raw1 = load_rows("raw1", w1, 0, H)
+        nc.sync.dma_start(offsets[:], offs)
         for q in range(4):
             nc.sync.dma_start(
                 out=table_scales[32 * q : 32 * q + 4, :].bitcast(I32),
@@ -117,23 +117,22 @@ def tile_picked_yenergy_dev_p_kernel(tc, x_words, x_scales, w1, w2, unit, wn, wd
         nc.vector.tensor_copy(picked_scales[:], table_scales[:].indirect(offsets[:]))
 
         woven1 = keep.tile([P, PACK, P, PACK], BF16, name="woven1", align_bytes=64)
-        deal(nc.vector.tensor_copy, woven1, 0, 16, raw1, 0)
-        deal(nc.scalar.copy, woven1, 16, P - 16, raw1, PACK * 16)
+        deal(nc.vector.tensor_copy, woven1, 0, 48, raw1, 0)
+        deal(nc.scalar.copy, woven1, 48, P - 48, raw1, PACK * 48)
         q1 = quantize_dealt("q1", woven1)
         nc.vector.tensor_copy(picked_words[:], table_words[:].bitcast(U32).indirect(offsets[:]))
 
-        sq1 = keep.tile([P, PACK, S], F32, name="sq1")
+        woven2 = keep.tile([P, PACK, P, PACK], BF16, name="woven2", align_bytes=64)
+        deal(nc.scalar.copy, woven2, 0, 64, raw2[0], 0)
+        deal(nc.vector.tensor_copy, woven2, 64, 64, raw2[1], 0)
+        q2 = planes("q2", H)
+        quantize(q2, 0, H, woven2[:].rearrange("p t m j -> p (t m j)"))
+
+        sq1 = keep.tile([P, PACK, S], F32, name="sq1", tag="raw2_0")
         for t in range(PACK):
             acc = psum.tile([P, S], F32, name="filters")
             mx(acc[:], q1, t * P, picked, 0, S)
             nc.scalar.activation(sq1[:, t, :], acc[:], ACT.Square, scale=unit_root[:, t : t + 1])
-
-        woven2 = keep.tile([P, PACK, P, PACK], BF16, name="woven2", align_bytes=64)
-        q2 = planes("q2", H)
-        for h in range(2):
-            deal(nc.vector.tensor_copy, woven2, h * 64, 64, raw2[h], 0)
-            for t in range(PACK):
-                quantize(q2, t * P + h * 64, 64, woven2[:, t, h * 64 : (h + 1) * 64, :].rearrange("p m j -> p (m j)"))
 
         def signed(name, raw):
             woven = keep.tile([P, N * PACK], BF16, name=name + "_woven", align_bytes=64)
@@ -195,6 +194,7 @@ def tile_picked_yenergy_dev_p_kernel(tc, x_words, x_scales, w1, w2, unit, wn, wd
 
         def rates(c, qe, c0, width, parts):
             num = keep.tile([P, 2 * width], F32, name="num_%d" % c)
+            size = keep.tile([P, 2 * width], F32, name="size_%d" % c)
             prod = keep.tile([P, 2 * width], F32, name="prod_%d" % c)
             drive = [psum.tile([P, width], F32, name="filters") for m in range(2)]
             norm = [psum.tile([P, width], F32, name="cells") for m in range(2)]
@@ -204,13 +204,14 @@ def tile_picked_yenergy_dev_p_kernel(tc, x_words, x_scales, w1, w2, unit, wn, wd
             for ms in parts:
                 for m in ms:
                     cols = slice(m * width, (m + 1) * width)
-                    nc.scalar.activation(num[:, cols], drive[m][:], ACT.Abs, scale=rmax_sb[:, m : m + 1])
+                    nc.scalar.activation(num[:, cols], drive[m][:], ACT.Identity, scale=rmax_sb[:, m : m + 1])
                     nc.vector.scalar_tensor_tensor(
                         prod[:, cols], norm[m][:], half_sb[:, m : m + 1], num[:, cols], ALU.add, ALU.mult
                     )
             for ms in parts:
                 cols = slice(ms[0] * width, (ms[-1] + 1) * width)
-                finish("rate_%d_%d" % (c, ms[0]), num[:, cols], prod[:, cols], ms, c0, width)
+                nc.scalar.activation(size[:, cols], num[:, cols], ACT.Abs)
+                finish("rate_%d_%d" % (c, ms[0]), size[:, cols], prod[:, cols], ms, c0, width)
 
         qn = signed("qn", rawn)
         qes = [energy(c, c0, width) for c, (c0, width) in enumerate(CHUNKS)]

from contextlib import ExitStack

import concourse.mybir as mybir

K, T, S, D, H, N = 512, 2048, 512, 4, 512, 256
FLOPS = 2 * K * H * S * 2 + 2 * H * N * S * 2

F32 = mybir.dt.float32
BF16 = mybir.dt.bfloat16
I32 = mybir.dt.int32
U32 = mybir.dt.uint32
U16 = mybir.dt.uint16
U8 = mybir.dt.uint8
FP8X4 = mybir.dt.float8_e4m3fn_x4
ACT = mybir.ActivationFunctionType
ALU = mybir.AluOpType
AX = mybir.AxisListType

P = 128
PACK = 4
HALF = 256
TINY = 2.0 ** -84
C2 = 2.0 ** (-2.0 / 3.0)
CHUNKS = ((0,128),(128,128),(256,256))


def tile_picked_yenergy_dev_p_kernel(tc, x_words, x_scales, w1, w2, unit, wn, wd, rmax, half, offs, out):
    nc = tc.nc
    with ExitStack() as ctx:
        keep = ctx.enter_context(tc.tile_pool(name="keep", bufs=1))
        psum = ctx.enter_context(tc.psum_pool(name="psum", bufs=4))

        offsets = keep.tile([P, S // 16], U16, name="offsets")
        table_words = keep.tile([P, T], I32, name="table_words", align_bytes=64)
        table_scales = keep.tile([P, T], U8, name="table_scales", tag="early", align_bytes=64)
        tiny = keep.tile([P, 1], F32, name="tiny")
        unit_sb = keep.tile([P, PACK], F32, name="unit_sb")
        rmax_sb = keep.tile([P, 2], F32, name="rmax_sb")
        half_sb = keep.tile([P, 2], F32, name="half_sb")

        nc.vector.memset(table_scales[:].bitcast(I32), 0)
        nc.gpsimd.memset(tiny[:], TINY)

        def load_rows(name, w, c0, width):
            raw = keep.tile([P, PACK, width], F32, name=name)
            nc.sync.dma_start(out=raw[:], in_=w.rearrange("(p j) c -> p j c", j=PACK)[:, :, c0 : c0 + width])
            return raw

        nc.sync.dma_start(out=unit_sb[:], in_=unit.rearrange("(p t) o -> p (t o)", t=PACK))
        raw1 = load_rows("raw1", w1, 0, H)
        nc.sync.dma_start(offsets[:], offs)
        for q in range(4):
            nc.sync.dma_start(
                out=table_scales[32 * q : 32 * q + 4, :].bitcast(I32),
                in_=x_scales[0][4 * q : 4 * q + 4, :].bitcast(I32),
            )
        nc.sync.dma_start(out=table_words[:], in_=x_words[0].rearrange("p n t -> p (n t)").bitcast(I32))
        raw2 = [load_rows("raw2_%d" % h, w2, h * HALF, HALF) for h in range(2)]
        rawd = load_rows("rawd", wd, 0, N)
        rawn = load_rows("rawn", wn, 0, N)
        with nc.allow_non_contiguous_dma(reason="one value a partition"):
            nc.sync.dma_start(out=rmax_sb[:], in_=rmax.rearrange("(m p) o -> p (m o)", p=P))
            nc.sync.dma_start(out=half_sb[:], in_=half.rearrange("(m p) o -> p (m o)", p=P))

        def minus_root_of_ratio(name, width, num, prod):
            inv, inv2, first, check, root = [
                keep.tile([P, width], F32, name=name + part) for part in ("_inv", "_inv2", "_first", "_check", "_root")
            ]
            nc.scalar.activation(inv[:], prod, ACT.Abs_reciprocal_sqrt, bias=tiny[:], scale=1.0 / C2)
            nc.scalar.activation(inv2[:], inv[:], ACT.Square)
            nc.vector.tensor_tensor(first[:], num, inv[:], ALU.mult)
            nc.vector.tensor_tensor(check[:], prod, inv2[:], ALU.mult)
            nc.vector.scalar_tensor_tensor(root[:], check[:], 3.0 * C2, first[:], ALU.subtract, ALU.mult)
            return root

        unit_abs = keep.tile([P, PACK], F32, name="unit_abs")
        unit_sign = keep.tile([P, PACK], F32, name="unit_sign")
        nc.vector.scalar_tensor_tensor(unit_abs[:], unit_sb[:], -1.0, unit_sb[:], ALU.mult, ALU.max)
        unit_root = minus_root_of_ratio("unit", PACK, unit_abs[:], unit_abs[:])
        nc.scalar.activation(unit_sign[:], unit_sb[:], ACT.Sign)

        def planes(name, width, tag=None):
            codes = keep.tile([P, width], U32, name=name + "_codes", tag=tag or name, align_bytes=64)
            scales = keep.tile([P, width], U8, name=name + "_scales", align_bytes=64)
            return codes, scales

        def quantize(dst, c0, width, woven):
            nc.vector.quantize_mx(
                out=dst[0][:, c0 : c0 + width].bitcast(FP8X4), scales=dst[1][:, c0 : c0 + width], in_=woven
            )

        def mx(acc, lhs, l0, rhs, r0, width):
            nc.tensor.matmul_mx(
                out=acc,
                lhsT=lhs[0][:, l0 : l0 + P].bitcast(FP8X4),
                lhsT_scale=lhs[1][:, l0 : l0 + P],
                rhs=rhs[0][:, r0 : r0 + width].bitcast(FP8X4),
                rhs_scale=rhs[1][:, r0 : r0 + width],
                start=True,
                stop=True,
            )

        def deal(copy, woven, m0, count, raw, c0):
            copy(
                woven[:, :, m0 : m0 + count, :].rearrange("p t m j -> p m t j"),
                raw[:, :, c0 : c0 + PACK * count].rearrange("p j (m t) -> p m t j", t=PACK),
            )

        def quantize_dealt(name, woven):
            q = planes(name, H, "early")
            quantize(q, 0, H, woven[:].rearrange("p t m j -> p (t m j)"))
            return q

        picked_words = keep.tile([P, S], U32, name="picked_words", align_bytes=64)
        picked_scales = keep.tile([P, S], U8, name="picked_scales", align_bytes=64)
        picked = (picked_words, picked_scales)
        nc.vector.tensor_copy(picked_scales[:], table_scales[:].indirect(offsets[:]))

        woven1 = keep.tile([P, PACK, P, PACK], BF16, name="woven1", align_bytes=64)
        deal(nc.vector.tensor_copy, woven1, 0, 48, raw1, 0)
        deal(nc.scalar.copy, woven1, 48, P - 48, raw1, PACK * 48)
        q1 = quantize_dealt("q1", woven1)
        nc.vector.tensor_copy(picked_words[:], table_words[:].bitcast(U32).indirect(offsets[:]))

        woven2 = keep.tile([P, PACK, P, PACK], BF16, name="woven2", align_bytes=64)
        deal(nc.scalar.copy, woven2, 0, 64, raw2[0], 0)
        deal(nc.vector.tensor_copy, woven2, 64, 64, raw2[1], 0)
        q2 = planes("q2", H)
        quantize(q2, 0, H, woven2[:].rearrange("p t m j -> p (t m j)"))

        sq1 = keep.tile([P, PACK, S], F32, name="sq1", tag="raw2_0")
        for t in range(PACK):
            acc = psum.tile([P, S], F32, name="filters")
            mx(acc[:], q1, t * P, picked, 0, S)
            nc.scalar.activation(sq1[:, t, :], acc[:], ACT.Square, scale=unit_root[:, t : t + 1])

        def signed(name, raw):
            woven = keep.tile([P, N * PACK], BF16, name=name + "_woven", align_bytes=64)
            nc.vector.tensor_tensor(
                woven[:].rearrange("p (c i j) -> p c j i", i=4, j=PACK),
                raw[:].rearrange("p j (c i) -> p c j i", i=4),
                unit_sign[:].unsqueeze(1).unsqueeze(3).to_broadcast([P, N // 4, PACK, 4]),
                ALU.mult,
            )
            q = planes(name, N)
            quantize(q, 0, N, woven[:])
            return q

        qd = signed("qd", rawd)

        def energy(c, c0, width):
            sq2 = keep.tile([P, PACK, width], F32, name="sq2_%d" % c)
            per_bank = S // width
            for t0 in range(0, PACK, per_bank):
                acc = psum.tile([P, per_bank, width], F32, name="filters")
                for t in range(per_bank):
                    mx(acc[:, t, :], q2, (t0 + t) * P, picked, c0, width)
                for t in range(per_bank):
                    nc.scalar.activation(
                        sq2[:, t0 + t, :], acc[:, t, :], ACT.Square, scale=unit_root[:, t0 + t : t0 + t + 1]
                    )
            e1 = keep.tile([P, width * PACK], BF16, name="e1_%d" % c, align_bytes=64)
            by_four = "p t (c i) -> p c t i"
            nc.vector.tensor_tensor(
                e1[:].rearrange("p (c i t) -> p c t i", i=4, t=PACK),
                sq1[:, :, c0 : c0 + width].rearrange(by_four, i=4),
                sq2[:].rearrange(by_four, i=4),
                ALU.add,
            )
            qe = planes("qe_%d" % c, width)
            quantize(qe, 0, width, e1[:])
            return qe

        def finish(name, num, prod, ms, c0, width):
            total = len(ms) * width
            rate = minus_root_of_ratio(name, total, num, prod)
            groups = total // D
            sums = keep.tile([P, groups], F32, name=name + "_sums")
            res = keep.tile([P, total], F32, name=name + "_res")
            by_group = "p (v d) -> p v d"
            nc.vector.tensor_reduce(sums[:], rate[:].rearrange(by_group, d=D), AX.X, ALU.add)
            nc.vector.scalar_tensor_tensor(
                res[:].rearrange(by_group, d=D),
                sums[:].unsqueeze(2).to_broadcast([P, groups, D]),
                1.0 / D,
                rate[:].rearrange(by_group, d=D),
                ALU.mult,
                ALU.subtract,
            )
            nc.sync.dma_start(
                out=out.rearrange("(m p) n -> p m n", p=P)[:, ms[0] : ms[-1] + 1, c0 : c0 + width],
                in_=res[:].rearrange("p (m n) -> p m n", m=len(ms)),
            )

        def rates(c, qe, c0, width, parts):
            num = keep.tile([P, 2 * width], F32, name="num_%d" % c)
            size = keep.tile([P, 2 * width], F32, name="size_%d" % c)
            prod = keep.tile([P, 2 * width], F32, name="prod_%d" % c)
            drive = [psum.tile([P, width], F32, name="filters") for m in range(2)]
            norm = [psum.tile([P, width], F32, name="cells") for m in range(2)]
            for m in range(2):
                mx(drive[m][:], qd, m * P, qe, 0, width)
                mx(norm[m][:], qn, m * P, qe, 0, width)
            for ms in parts:
                for m in ms:
                    cols = slice(m * width, (m + 1) * width)
                    nc.scalar.activation(num[:, cols], drive[m][:], ACT.Identity, scale=rmax_sb[:, m : m + 1])
                    nc.vector.scalar_tensor_tensor(
                        prod[:, cols], norm[m][:], half_sb[:, m : m + 1], num[:, cols], ALU.add, ALU.mult
                    )
            for ms in parts:
                cols = slice(ms[0] * width, (ms[-1] + 1) * width)
                nc.scalar.activation(size[:, cols], num[:, cols], ACT.Abs)
                finish("rate_%d_%d" % (c, ms[0]), size[:, cols], prod[:, cols], ms, c0, width)

        qn = signed("qn", rawn)
        qes = [energy(c, c0, width) for c, (c0, width) in enumerate(CHUNKS)]
        for c, (c0, width) in enumerate(CHUNKS):
            rates(c, qes[c], c0, width, [(0, 1)] if width == P else [(0,), (1,)])
